import numpy as np
import ml_dtypes


def mxq(x, axis, fmt="e4m3"):
    dtype, down = {"e4m3": (ml_dtypes.float8_e4m3fn, 7), "e5m2": (ml_dtypes.float8_e5m2, 14)}[fmt]
    v = np.moveaxis(np.asarray(x, np.float32).astype(ml_dtypes.bfloat16).astype(np.float64), axis, -1)
    blocks = v.reshape(v.shape[:-1] + (-1, 32))
    amax = np.abs(blocks).max(-1, keepdims=True)
    byte = np.maximum(np.where(amax > 0, np.frexp(amax)[1] - 1 + 127, 0) - down, 1)
    scale = np.exp2(byte - 127.0)
    codes = (blocks / scale).astype(np.float32).astype(dtype).astype(np.float64)
    return np.moveaxis((codes * scale).reshape(v.shape), -1, axis)


WIDE = False


def mx_kscale(k):
    if not WIDE:
        return np.ones(k)
    levels = np.array([30, -30])
    if k % 512:
        return np.exp2(np.random.permutation(np.resize(levels, k // 32))).repeat(32)
    a = np.empty((k // 512, 16))
    for p in range(k // 512):
        a[p, :8] = np.random.permutation(np.resize(levels, 8))
        for g in range(8):
            far = levels[np.abs(levels - a[p, g]) >= 10]
            a[p, g + 8] = far[np.random.randint(len(far))]
    return np.exp2(a.ravel()).repeat(32)


def f64(x):
    return np.asarray(x).astype(np.float64)


def striped(idx):
    return np.tile(np.asarray(idx).reshape(-1, 16).T, (8, 1)).astype(np.uint16)


def unstriped(offs):
    return offs[:16].T.reshape(-1).astype(np.int64)


E2M1 = np.array([0.0, 0.5, 1.0, 1.5, 2.0, 3.0, 4.0, 6.0, -0.0, -0.5, -1.0, -1.5, -2.0, -3.0, -4.0, -6.0])


def pack_weight(w, fmt):
    k, n = w.shape
    w = f64(np.asarray(w, np.float32).astype(ml_dtypes.bfloat16)).reshape(k // 32, 32, n)
    amax = np.abs(w).max(1)
    if fmt == "e4m3":
        byte = np.frexp(amax)[1] - 1 + 127 - 7
    else:
        mant, ex = np.frexp(amax / 6.0)
        byte = np.where(mant > 0.5, ex, ex - 1) + 127
    byte = np.clip(np.where(amax > 0, byte, 1), 1, 254)
    scaled = (w * np.exp2(127.0 - byte)[:, None, :]).reshape(k, n).astype(np.float32)
    by_word = np.ascontiguousarray(scaled.reshape(k // 512, 128, 4, n).transpose(0, 1, 3, 2))
    if fmt == "e4m3":
        words = by_word.astype(ml_dtypes.float8_e4m3fn).view(np.uint8)
    else:
        c = by_word.astype(ml_dtypes.float4_e2m1fn).view(np.uint8) & 0xF
        words = (c[..., 0::2] | (c[..., 1::2] << 4)).reshape(k // 512, 128, 2 * n)
    return np.ascontiguousarray(words), np.ascontiguousarray(byte.astype(np.uint8).reshape(k // 512, 16, n))


def unpack_weight(words, scales, fmt):
    g, _, n = scales.shape
    words = np.ascontiguousarray(words).reshape(g, 128, n, -1)
    if fmt == "e4m3":
        vals = words.view(ml_dtypes.float8_e4m3fn).astype(np.float64)
    else:
        nib = np.empty((g, 128, n, 4), np.uint8)
        nib[..., 0::2] = words & 0xF
        nib[..., 1::2] = words >> 4
        vals = E2M1[nib]
    vals = vals * np.repeat(np.exp2(scales.astype(np.float64) - 127.0), 8, axis=1)[..., None]
    return vals.transpose(0, 1, 3, 2).reshape(g * 512, n)


def sigmoid(v):
    return 1.0 / (1.0 + np.exp(-v))


def sgn(shape):
    return np.random.uniform(0.5, 2.0, shape) * np.where(np.random.standard_normal(shape) < 0, -1.0, 1.0)


K, T, J, R, F, Z, O, U, D, N, L, E = 512, 1024, 256, 512, 512, 1024, 128, 128, 256, 256, 512, 1024


def setup_inputs():
    n = np.random.standard_normal
    idx = np.random.permutation(T)[:J]
    idx2 = np.random.permutation(Z)[:J]
    idx3 = np.random.permutation(J)[:O]
    idx4 = np.random.permutation(J)[:O]
    idx5 = np.random.permutation(J)[:U]
    idx6 = np.random.permutation(J)[:U]
    idx7 = np.random.permutation(E)[:D]
    ff = mx_kscale(F)
    fk = mx_kscale(K)
    fr = mx_kscale(R)
    fl = mx_kscale(L)
    xop = pack_weight(n((F, Z)) / ff[:, None], "e4m3")
    wp = pack_weight(n((K, R)) * 1 / np.sqrt(K) / fk[:, None], "e4m3")
    w2p = pack_weight(n((F, R)) * 1 / np.sqrt(F) * ff[:, None], "e2m1")
    wbp = pack_weight(n((R, N)) * 1 / np.sqrt(R) / fr[:, None], "e2m1")
    sxp = pack_weight(n((L, D)) / fl[:, None], "e4m3")
    wsp = pack_weight(n((L, N)) * 1 / np.sqrt(L) * fl[:, None], "e4m3")
    return {
        "xo_words": xop[0],
        "xo_scales": xop[1],
        "cq": (np.random.randint(-7, 8, (K, T)).astype(np.float64)).astype(np.float32),
        "gs": (np.random.uniform(0.1, 0.4, (K, 1)) * fk[:, None]).astype(np.float32),
        "w_words": wp[0],
        "w_scales": wp[1],
        "w2_words": w2p[0],
        "w2_scales": w2p[1],
        "sa": (np.random.uniform(0.5, 1.6, (R, 1)) * fr[:, None]).astype(np.float32),
        "sb": (np.random.uniform(0.5, 1.6, (R, 1)) * fr[:, None]).astype(np.float32),
        "sg": (sgn((R, 1))).astype(np.float32),
        "bg": (np.random.uniform(-2.0, 2.0, (R, 1))).astype(np.float32),
        "sh": (sgn((R, 1))).astype(np.float32),
        "bh": (np.random.uniform(-2.0, 2.0, (R, 1))).astype(np.float32),
        "wb_words": wbp[0],
        "wb_scales": wbp[1],
        "sx_words": sxp[0],
        "sx_scales": sxp[1],
        "ws_words": wsp[0],
        "ws_scales": wsp[1],
        "offs": striped(idx),
        "offs2": striped(idx2),
        "offs3": striped(idx3),
        "offs4": striped(idx4),
        "offs5": striped(idx5),
        "offs6": striped(idx6),
        "offs7": striped(idx7),
    }


def reference(xo_words, xo_scales, cq, gs, w_words, w_scales, w2_words, w2_scales, sa, sb, sg, bg, sh, bh, wb_words, wb_scales, sx_words, sx_scales, ws_words, ws_scales, offs, offs2, offs3, offs4, offs5, offs6, offs7):
    idx = unstriped(offs)
    idx2 = unstriped(offs2)
    idx3 = unstriped(offs3)
    idx4 = unstriped(offs4)
    idx5 = unstriped(offs5)
    idx6 = unstriped(offs6)
    idx7 = unstriped(offs7)
    xou = unpack_weight(xo_words, xo_scales, "e4m3")
    wu = unpack_weight(w_words, w_scales, "e4m3")
    w2u = unpack_weight(w2_words, w2_scales, "e2m1")
    wbu = unpack_weight(wb_words, wb_scales, "e2m1")
    sxu = unpack_weight(sx_words, sx_scales, "e4m3")
    wsu = unpack_weight(ws_words, ws_scales, "e4m3")
    x1 = f64(cq)[:, idx] * f64(gs)
    x1q = mxq(x1, 0, "e4m3")
    a = wu.T @ x1q
    xoidx2g = xou[:, idx2]
    b = w2u.T @ xoidx2g
    h1 = a[:, idx3] * f64(sa) * sigmoid(a[:, idx4] * f64(sg) + f64(bg))
    h2 = b[:, idx5] * f64(sb) * sigmoid(b[:, idx6] * f64(sh) + f64(bh))
    hid = np.concatenate([h1, h2], axis=1)
    hidq = mxq(hid, 0, "e5m2")
    p = wbu.T @ hidq + wsu.T @ sxu
    y = np.zeros((N, E))
    y[:, idx7] = p
    return y

@@ -1,0 +1,226 @@
+from contextlib import ExitStack
+
+import concourse.mybir as mybir
+
+F32 = mybir.dt.float32
+BF16 = mybir.dt.bfloat16
+I32 = mybir.dt.int32
+U32 = mybir.dt.uint32
+U16 = mybir.dt.uint16
+U8 = mybir.dt.uint8
+E4M3 = mybir.dt.float8_e4m3fn_x4
+E5M2 = mybir.dt.float8_e5m2_x4
+E2M1 = mybir.dt.float4_e2m1fn_x4
+COPY = mybir.ActivationFunctionType.Copy
+SIGMOID = mybir.ActivationFunctionType.Sigmoid
+MULT = mybir.AluOpType.mult
+
+P = 128
+PACK = 4
+QUAD = 32
+TABLE = 1024
+SLOTS = 256
+HIDDEN = 512
+PLACES = 128
+OUT_ROWS = 256
+PAGE = 1024
+
+FLOPS = 2 * 512 * (2 * HIDDEN * SLOTS + 2 * OUT_ROWS * 2 * PLACES)
+
+
+def tile_list_gatedsides_codednote_further_scattered_kernel(
+    tc, xo_words, xo_scales, cq, gs, w_words, w_scales, w2_words, w2_scales, sa, sb, sg, bg, sh, bh,
+    wb_words, wb_scales, sx_words, sx_scales, ws_words, ws_scales,
+    offs, offs2, offs3, offs4, offs5, offs6, offs7, out,
+):
+    nc = tc.nc
+    with ExitStack() as ctx:
+        pool = ctx.enter_context(tc.tile_pool(name="keep", bufs=1))
+        psum = ctx.enter_context(tc.psum_pool(name="psum", bufs=1))
+
+        def load_list(src, name):
+            tile = pool.tile(list(src.shape), U16, name=name)
+            nc.sync.dma_start(tile[:], src)
+            return tile
+
+        def load_words(src, dtype, columns, name):
+            tile = pool.tile([P, columns], dtype, name=name, align_bytes=64)
+            nc.sync.dma_start(tile[:].bitcast(I32), src.bitcast(I32))
+            return tile
+
+        def load_scale_rows(dst, src):
+            nc.sync.dma_start(dst, src[0].bitcast(I32).rearrange("(q r) w -> r q w", r=PACK))
+
+        def load_rows(src, name):
+            tile = pool.tile([P, PACK], F32, name=name)
+            nc.sync.dma_start(tile[:], src.rearrange("(p t) o -> p (t o)", t=PACK))
+            return tile
+
+        def load_plane(t):
+            tile = pool.tile([P, TABLE], F32, name="cq_plane%d" % t, tag="cq_plane%d" % t)
+            nc.sync.dma_start(tile[:], cq.rearrange("(p t) c -> p t c", t=PACK)[:, t, :])
+            return tile
+
+        def flat(words):
+            return words[0].rearrange("p n t -> p (n t)")
+
+        up_stage = pool.tile([P, PACK, HIDDEN // 4], I32, name="up_stage")
+        nc.vector.memset(up_stage[64:96], 0)
+        xo_plane = pool.tile([P, TABLE], U8, name="xo_plane")
+        nc.vector.memset(xo_plane[:].bitcast(I32), 0)
+        down_stage = pool.tile([P, PACK, OUT_ROWS // 4], I32, name="down_stage")
+        nc.vector.memset(down_stage[64:96], 0)
+
+        xo_stage = pool.tile([PACK, PACK, TABLE // 4], I32, name="xo_stage")
+        load_scale_rows(xo_stage[:], xo_scales)
+        list2 = load_list(offs2, "list2")
+        xo_table = load_words(flat(xo_words), U32, TABLE, "xo_table")
+        load_scale_rows(up_stage[64:68], w2_scales)
+        load_scale_rows(up_stage[68:72], w_scales)
+        w2_raw = load_words(w2_words[0], U16, HIDDEN, "w2_raw")
+        planes = [load_plane(0)]
+        list1 = load_list(offs, "list1")
+        gs_t = load_rows(gs, "gs_t")
+        list6 = load_list(offs6, "list6")
+        planes.append(load_plane(1))
+        list5 = load_list(offs5, "list5")
+        sh_t = load_rows(sh, "sh_t")
+        bh_t = load_rows(bh, "bh_t")
+        sb_t = load_rows(sb, "sb_t")
+        planes.extend([load_plane(2), load_plane(3)])
+        w_raw = load_words(flat(w_words), U32, HIDDEN, "w_raw")
+        load_scale_rows(down_stage[64:68], wb_scales)
+        load_scale_rows(down_stage[68:72], sx_scales)
+        load_scale_rows(down_stage[72:76], ws_scales)
+        wb_codes = load_words(wb_words[0], U16, OUT_ROWS, "wb_codes")
+        list4 = load_list(offs4, "list4")
+        list3 = load_list(offs3, "list3")
+        sg_t = load_rows(sg, "sg_t")
+        bg_t = load_rows(bg, "bg_t")
+        sa_t = load_rows(sa, "sa_t")
+        ws_codes = load_words(flat(ws_words), U32, OUT_ROWS, "ws_codes")
+        sx_codes = load_words(flat(sx_words), U32, 2 * PLACES, "sx_codes")
+        list7 = load_list(offs7, "list7")
+
+        def spread(plane, stage, first, rows):
+            for q in range(PACK):
+                nc.vector.tensor_copy(
+                    plane[QUAD * q : QUAD * q + rows, :].bitcast(I32), stage[first : first + rows, q, :]
+                )
+
+        spread(xo_plane, xo_stage, 0, PACK)
+        up_raw = pool.tile([P, HIDDEN], U8, name="up_raw")
+        spread(up_raw, up_stage, 64, QUAD)
+        xo_codes = pool.tile([P, SLOTS], U32, name="xo_codes", align_bytes=64)
+        nc.vector.tensor_copy(xo_codes[:], xo_table[:].indirect(list2[:]))
+        xo_picked = pool.tile([P, SLOTS], U8, name="xo_picked", align_bytes=64)
+        nc.vector.tensor_copy(xo_picked[:], xo_plane[:].indirect(list2[:]))
+        up_plane = pool.tile([P, HIDDEN], U8, name="up_plane", align_bytes=64)
+        nc.vector.tensor_copy(
+            up_plane[:].rearrange("p (t m) -> p t m", t=PACK), up_raw[:].rearrange("p (m t) -> p t m", t=PACK)
+        )
+        w2_codes = pool.tile([P, HIDDEN], U16, name="w2_codes", align_bytes=64)
+        nc.scalar.copy(
+            w2_codes[:].rearrange("p (t m) -> p t m", t=PACK), w2_raw[:].rearrange("p (m t) -> p t m", t=PACK)
+        )
+
+        def first_stage(name, lhs_codes, lhs_dtype, lhs_plane, rhs_codes, rhs_plane):
+            rows = []
+            for t in range(PACK):
+                cols = slice(t * P, (t + 1) * P)
+                bank = psum.tile([P, SLOTS], F32, name="stage1_%d" % t)
+                nc.tensor.matmul_mx(
+                    bank[:], lhsT=lhs_codes[:, cols].bitcast(lhs_dtype), lhsT_scale=lhs_plane[:, cols],
+                    rhs=rhs_codes[:].bitcast(E4M3), rhs_scale=rhs_plane[:], start=True, stop=True,
+                )
+                tile = pool.tile([P, SLOTS], F32, name="%s%d" % (name, t), tag="%s%d" % (name, t), align_bytes=64)
+                nc.vector.tensor_copy(tile[:], bank[:])
+                rows.append(tile)
+            return rows
+
+        def gated(name, rows, value_list, weight, gate_list, slope, offset, woven_tag, pair_tags):
+            woven = pool.tile([P, PLACES, PACK], BF16, name=name + "_woven", tag=woven_tag, align_bytes=64)
+            for pair in range(2):
+                both = pool.tile([P, 2, 2, PLACES], F32, name="%s_pair%d" % (name, pair), tag=pair_tags[pair])
+                value, gate = both[:, 0], both[:, 1]
+                for e in range(2):
+                    t = 2 * pair + e
+                    nc.scalar.activation(
+                        gate[:, e, :], rows[t][:].indirect(gate_list[:]), SIGMOID,
+                        bias=offset[:, t : t + 1], scale=slope[:, t : t + 1],
+                    )
+                    nc.scalar.activation(
+                        value[:, e, :], rows[t][:].indirect(value_list[:]), COPY, scale=weight[:, t : t + 1]
+                    )
+                nc.vector.tensor_tensor(
+                    woven[:, :, 2 * pair : 2 * pair + 2],
+                    value.rearrange("p e o -> p o e"), gate.rearrange("p e o -> p o e"), MULT,
+                )
+            codes = pool.tile([P, PLACES], U32, name=name + "_codes", align_bytes=64)
+            plane = pool.tile([P, PLACES], U8, name=name + "_plane", align_bytes=64)
+            nc.vector.quantize_mx(codes[:].bitcast(E5M2), plane[:], woven[:].rearrange("p o t -> p (o t)"))
+            return codes, plane
+
+        b_rows = first_stage("b_rows", w2_codes, E2M1, up_plane, xo_codes, xo_picked)
+
+        x1_woven = pool.tile([P, SLOTS, PACK], BF16, name="x1_woven", tag="x1_woven", align_bytes=64)
+        for pair in range(2):
+            picked = pool.tile([P, 2, SLOTS], BF16, name="x1_pair%d" % pair)
+            for e in range(2):
+                t = 2 * pair + e
+                nc.scalar.activation(picked[:, e, :], planes[t][:].indirect(list1[:]), COPY, scale=gs_t[:, t : t + 1])
+            nc.vector.tensor_copy(x1_woven[:, :, 2 * pair : 2 * pair + 2], picked[:].rearrange("p e j -> p j e"))
+        x1_codes = pool.tile([P, SLOTS], U32, name="x1_codes", align_bytes=64)
+        x1_plane = pool.tile([P, SLOTS], U8, name="x1_plane", align_bytes=64)
+        nc.vector.quantize_mx(x1_codes[:].bitcast(E4M3), x1_plane[:], x1_woven[:].rearrange("p j t -> p (j t)"))
+        w_codes = pool.tile([P, HIDDEN], U32, name="w_codes", align_bytes=64)
+        nc.vector.tensor_copy(
+            w_codes[:].rearrange("p (t m) -> p t m", t=PACK), w_raw[:].rearrange("p (m t) -> p t m", t=PACK)
+        )
+        a_rows = first_stage("a_rows", w_codes, E4M3, up_plane[4:], x1_codes, x1_plane)
+
+        h2_codes, h2_plane = gated("h2", b_rows, list5, sb_t, list6, sh_t, bh_t, "x1_woven", ("h2_pair0", "cq_plane3"))
+
+        down_plane = pool.tile([P, OUT_ROWS], U8, name="down_plane", align_bytes=64)
+        spread(down_plane, down_stage, 64, QUAD)
+        pages = []
+        for nt in range(2):
+            page = pool.tile([P, PAGE], F32, name="page%d" % nt)
+            nc.vector.memset(page[:], 0.0)
+            pages.append(page)
+
+        def second_stage(half, codes, plane):
+            d_cols = slice(half * PLACES, (half + 1) * PLACES)
+            banks = []
+            for nt in range(2):
+                n_cols = slice(nt * P, (nt + 1) * P)
+                bank = psum.tile([P, PLACES], F32, name="stage2_%d_%d" % (half, nt))
+                nc.tensor.matmul_mx(
+                    bank[:], lhsT=ws_codes[:, n_cols].bitcast(E4M3), lhsT_scale=down_plane[8:, n_cols],
+                    rhs=sx_codes[:, d_cols].bitcast(E4M3), rhs_scale=down_plane[4:, d_cols], start=True, stop=False,
+                )
+                nc.tensor.matmul_mx(
+                    bank[:], lhsT=wb_codes[:, n_cols].bitcast(E2M1), lhsT_scale=down_plane[:, n_cols],
+                    rhs=codes[:].bitcast(E5M2), rhs_scale=plane[:], start=False, stop=True,
+                )
+                banks.append(bank)
+            return banks
+
+        def place(half, nt, bank, tag):
+            places = list7[:, half * (PLACES // 16) : (half + 1) * (PLACES // 16)]
+            result = pool.tile([P, PLACES], F32, name="result_%d_%d" % (half, nt), tag=tag, align_bytes=64)
+            if nt == 0:
+                nc.vector.tensor_copy(result[:], bank[:])
+                nc.vector.tensor_copy(pages[nt][:].indirect(places), result[:])
+            else:
+                nc.scalar.copy(result[:], bank[:])
+                nc.scalar.activation(pages[nt][:].indirect(places), result[:], COPY)
+
+        late_banks = second_stage(1, h2_codes, h2_plane)
+        place(1, 0, late_banks[0], "late_result0")
+        h1_codes, h1_plane = gated("h1", a_rows, list3, sa_t, list4, sg_t, bg_t, "late_result0", ("h1_pair0", "h1_pair1"))
+        place(1, 1, late_banks[1], "a_rows3")
+        early_banks = second_stage(0, h1_codes, h1_plane)
+        for nt in range(2):
+            place(0, nt, early_banks[nt], "early_result%d" % nt)
+            nc.sync.dma_start(out[nt * P : (nt + 1) * P, :], pages[nt][:])

@@ -53,7 +53,7 @@ def tile_list_gatedsides_codednote_further_scattered_kernel(
 
         def load_rows(src, name):
             tile = pool.tile([P, PACK], F32, name=name)
-            nc.sync.dma_start(tile[:], src.rearrange("(p t) o -> p (t o)", t=PACK))
+            nc.gpsimd.dma_start(tile[:], src.rearrange("(p t) o -> p (t o)", t=PACK))
             return tile
 
         def load_plane(t):
@@ -71,36 +71,40 @@ def tile_list_gatedsides_codednote_further_scattered_kernel(
         down_stage = pool.tile([P, PACK, OUT_ROWS // 4], I32, name="down_stage")
         nc.vector.memset(down_stage[64:96], 0)
 
+        warm_in = pool.tile([P, 1], F32, name="warm_in")
+        nc.vector.memset(warm_in[:], 0.0)
+        warm_out = pool.tile([P, 1], F32, name="warm_out")
+        nc.scalar.activation(warm_out[:], warm_in[:], SIGMOID)
+        planes = [load_plane(0)]
+        load_scale_rows(up_stage[64:68], w2_scales)
+        load_scale_rows(up_stage[68:72], w_scales)
+        list1 = load_list(offs, "list1")
         xo_stage = pool.tile([PACK, PACK, TABLE // 4], I32, name="xo_stage")
         load_scale_rows(xo_stage[:], xo_scales)
         list2 = load_list(offs2, "list2")
         xo_table = load_words(flat(xo_words), U32, TABLE, "xo_table")
-        load_scale_rows(up_stage[64:68], w2_scales)
-        load_scale_rows(up_stage[68:72], w_scales)
-        w2_raw = load_words(w2_words[0], U16, HIDDEN, "w2_raw")
-        planes = [load_plane(0)]
-        list1 = load_list(offs, "list1")
-        gs_t = load_rows(gs, "gs_t")
-        list6 = load_list(offs6, "list6")
         planes.append(load_plane(1))
-        list5 = load_list(offs5, "list5")
-        sh_t = load_rows(sh, "sh_t")
-        bh_t = load_rows(bh, "bh_t")
-        sb_t = load_rows(sb, "sb_t")
+        w2_raw = load_words(w2_words[0], U16, HIDDEN, "w2_raw")
         planes.extend([load_plane(2), load_plane(3)])
+        list6 = load_list(offs6, "list6")
+        list5 = load_list(offs5, "list5")
         w_raw = load_words(flat(w_words), U32, HIDDEN, "w_raw")
         load_scale_rows(down_stage[64:68], wb_scales)
         load_scale_rows(down_stage[68:72], sx_scales)
         load_scale_rows(down_stage[72:76], ws_scales)
-        wb_codes = load_words(wb_words[0], U16, OUT_ROWS, "wb_codes")
         list4 = load_list(offs4, "list4")
         list3 = load_list(offs3, "list3")
-        sg_t = load_rows(sg, "sg_t")
-        bg_t = load_rows(bg, "bg_t")
-        sa_t = load_rows(sa, "sa_t")
+        wb_codes = load_words(wb_words[0], U16, OUT_ROWS, "wb_codes")
         ws_codes = load_words(flat(ws_words), U32, OUT_ROWS, "ws_codes")
         sx_codes = load_words(flat(sx_words), U32, 2 * PLACES, "sx_codes")
         list7 = load_list(offs7, "list7")
+        gs_t = load_rows(gs, "gs_t")
+        sh_t = load_rows(sh, "sh_t")
+        bh_t = load_rows(bh, "bh_t")
+        sb_t = load_rows(sb, "sb_t")
+        sg_t = load_rows(sg, "sg_t")
+        bg_t = load_rows(bg, "bg_t")
+        sa_t = load_rows(sa, "sa_t")
 
         def spread(plane, stage, first, rows):
             for q in range(PACK):
@@ -128,7 +132,7 @@ def tile_list_gatedsides_codednote_further_scattered_kernel(
             rows = []
             for t in range(PACK):
                 cols = slice(t * P, (t + 1) * P)
-                bank = psum.tile([P, SLOTS], F32, name="stage1_%d" % t)
+                bank = psum.tile([P, SLOTS], F32, name="%s_bank%d" % (name, t), tag="bank%d" % t)
                 nc.tensor.matmul_mx(
                     bank[:], lhsT=lhs_codes[:, cols].bitcast(lhs_dtype), lhsT_scale=lhs_plane[:, cols],
                     rhs=rhs_codes[:].bitcast(E4M3), rhs_scale=rhs_plane[:], start=True, stop=True,
@@ -138,11 +142,10 @@ def tile_list_gatedsides_codednote_further_scattered_kernel(
                 rows.append(tile)
             return rows
 
-        def gated(name, rows, value_list, weight, gate_list, slope, offset, woven_tag, pair_tags):
+        def gated(name, rows, value_list, weight, gate_list, slope, offset, woven_tag, picks):
             woven = pool.tile([P, PLACES, PACK], BF16, name=name + "_woven", tag=woven_tag, align_bytes=64)
             for pair in range(2):
-                both = pool.tile([P, 2, 2, PLACES], F32, name="%s_pair%d" % (name, pair), tag=pair_tags[pair])
-                value, gate = both[:, 0], both[:, 1]
+                value, gate = picks[pair][:, 0], picks[pair][:, 1]
                 for e in range(2):
                     t = 2 * pair + e
                     nc.scalar.activation(
@@ -170,7 +173,7 @@ def tile_list_gatedsides_codednote_further_scattered_kernel(
                 t = 2 * pair + e
                 nc.scalar.activation(picked[:, e, :], planes[t][:].indirect(list1[:]), COPY, scale=gs_t[:, t : t + 1])
             nc.vector.tensor_copy(x1_woven[:, :, 2 * pair : 2 * pair + 2], picked[:].rearrange("p e j -> p j e"))
-        x1_codes = pool.tile([P, SLOTS], U32, name="x1_codes", align_bytes=64)
+        x1_codes = pool.tile([P, SLOTS], U32, name="x1_codes", tag="x1_codes", align_bytes=64)
         x1_plane = pool.tile([P, SLOTS], U8, name="x1_plane", align_bytes=64)
         nc.vector.quantize_mx(x1_codes[:].bitcast(E4M3), x1_plane[:], x1_woven[:].rearrange("p j t -> p (j t)"))
         w_codes = pool.tile([P, HIDDEN], U32, name="w_codes", align_bytes=64)
@@ -179,9 +182,10 @@ def tile_list_gatedsides_codednote_further_scattered_kernel(
         )
         a_rows = first_stage("a_rows", w_codes, E4M3, up_plane[4:], x1_codes, x1_plane)
 
-        h2_codes, h2_plane = gated("h2", b_rows, list5, sb_t, list6, sh_t, bh_t, "x1_woven", ("h2_pair0", "cq_plane3"))
+        h2_picks = pool.tile([P, 2, 2, 2, PLACES], F32, name="h2_picks", tag="cq_plane3")
+        h2_codes, h2_plane = gated("h2", b_rows, list5, sb_t, list6, sh_t, bh_t, "x1_codes", (h2_picks[:, 0], h2_picks[:, 1]))
 
-        down_plane = pool.tile([P, OUT_ROWS], U8, name="down_plane", align_bytes=64)
+        down_plane = pool.tile([P, OUT_ROWS], U8, name="down_plane", tag="x1_woven", align_bytes=64)
         spread(down_plane, down_stage, 64, QUAD)
         pages = []
         for nt in range(2):
@@ -189,38 +193,38 @@ def tile_list_gatedsides_codednote_further_scattered_kernel(
             nc.vector.memset(page[:], 0.0)
             pages.append(page)
 
-        def second_stage(half, codes, plane):
+        def second_stage(half, nt, codes, plane, sums):
             d_cols = slice(half * PLACES, (half + 1) * PLACES)
-            banks = []
-            for nt in range(2):
-                n_cols = slice(nt * P, (nt + 1) * P)
-                bank = psum.tile([P, PLACES], F32, name="stage2_%d_%d" % (half, nt))
-                nc.tensor.matmul_mx(
-                    bank[:], lhsT=ws_codes[:, n_cols].bitcast(E4M3), lhsT_scale=down_plane[8:, n_cols],
-                    rhs=sx_codes[:, d_cols].bitcast(E4M3), rhs_scale=down_plane[4:, d_cols], start=True, stop=False,
-                )
-                nc.tensor.matmul_mx(
-                    bank[:], lhsT=wb_codes[:, n_cols].bitcast(E2M1), lhsT_scale=down_plane[:, n_cols],
-                    rhs=codes[:].bitcast(E5M2), rhs_scale=plane[:], start=False, stop=True,
-                )
-                banks.append(bank)
-            return banks
+            n_cols = slice(nt * P, (nt + 1) * P)
+            nc.tensor.matmul_mx(
+                sums, lhsT=ws_codes[:, n_cols].bitcast(E4M3), lhsT_scale=down_plane[8:, n_cols],
+                rhs=sx_codes[:, d_cols].bitcast(E4M3), rhs_scale=down_plane[4:, d_cols], start=True, stop=False,
+            )
+            nc.tensor.matmul_mx(
+                sums, lhsT=wb_codes[:, n_cols].bitcast(E2M1), lhsT_scale=down_plane[:, n_cols],
+                rhs=codes[:].bitcast(E5M2), rhs_scale=plane[:], start=False, stop=True,
+            )
 
-        def place(half, nt, bank, tag):
-            places = list7[:, half * (PLACES // 16) : (half + 1) * (PLACES // 16)]
-            result = pool.tile([P, PLACES], F32, name="result_%d_%d" % (half, nt), tag=tag, align_bytes=64)
+        def places(half):
+            return list7[:, half * (PLACES // 16) : (half + 1) * (PLACES // 16)]
+
+        late_bank = psum.tile([P, 2, PLACES], F32, name="late_bank", tag="bank3")
+        for nt in range(2):
+            second_stage(1, nt, h2_codes, h2_plane, late_bank[:, nt, :])
+        h1_picks = [pool.tile([P, 2, 2, PLACES], F32, name="h1_picks%d" % pair) for pair in range(2)]
+        h1_codes, h1_plane = gated("h1", a_rows, list3, sa_t, list4, sg_t, bg_t, "h1_woven", h1_picks)
+        late_result = pool.tile([P, 2, PLACES], F32, name="late_result", tag="a_rows3", align_bytes=64)
+        nc.scalar.copy(late_result[:], late_bank[:])
+        for nt in range(2):
+            nc.scalar.activation(pages[nt][:].indirect(places(1)), late_result[:, nt, :], COPY)
+        for nt in range(2):
+            bank = psum.tile([P, PLACES], F32, name="early_bank%d" % nt, tag="bank%d" % (1 + nt))
+            second_stage(0, nt, h1_codes, h1_plane, bank[:])
+            result = pool.tile([P, PLACES], F32, name="early_result%d" % nt)
             if nt == 0:
                 nc.vector.tensor_copy(result[:], bank[:])
-                nc.vector.tensor_copy(pages[nt][:].indirect(places), result[:])
+                nc.vector.tensor_copy(pages[nt][:].indirect(places(0)), result[:])
             else:
                 nc.scalar.copy(result[:], bank[:])
-                nc.scalar.activation(pages[nt][:].indirect(places), result[:], COPY)
-
-        late_banks = second_stage(1, h2_codes, h2_plane)
-        place(1, 0, late_banks[0], "late_result0")
-        h1_codes, h1_plane = gated("h1", a_rows, list3, sa_t, list4, sg_t, bg_t, "late_result0", ("h1_pair0", "h1_pair1"))
-        place(1, 1, late_banks[1], "a_rows3")
-        early_banks = second_stage(0, h1_codes, h1_plane)
-        for nt in range(2):
-            place(0, nt, early_banks[nt], "early_result%d" % nt)
+                nc.scalar.activation(pages[nt][:].indirect(places(0)), result[:], COPY)
             nc.sync.dma_start(out[nt * P : (nt + 1) * P, :], pages[nt][:])

@@ -18,14 +18,18 @@ MULT = mybir.AluOpType.mult
 P = 128
 PACK = 4
 QUAD = 32
+CONTRACTION = P * PACK
 TABLE = 1024
 SLOTS = 256
 HIDDEN = 512
 PLACES = 128
 OUT_ROWS = 256
 PAGE = 1024
+PER_COLUMN = 16
+STAGE = 2 * QUAD
+EARLY, LATE = 0, 1
 
-FLOPS = 2 * 512 * (2 * HIDDEN * SLOTS + 2 * OUT_ROWS * 2 * PLACES)
+FLOPS = 2 * CONTRACTION * (2 * HIDDEN * SLOTS + 2 * OUT_ROWS * 2 * PLACES)
 
 
 def tile_list_gatedsides_codednote_further_scattered_kernel(
@@ -51,60 +55,64 @@ def tile_list_gatedsides_codednote_further_scattered_kernel(
         def load_scale_rows(dst, src):
             nc.sync.dma_start(dst, src[0].bitcast(I32).rearrange("(q r) w -> r q w", r=PACK))
 
-        def load_rows(src, name):
+        def load_per_row(src, name, queue):
             tile = pool.tile([P, PACK], F32, name=name)
-            nc.gpsimd.dma_start(tile[:], src.rearrange("(p t) o -> p (t o)", t=PACK))
+            queue.dma_start(tile[:], src.rearrange("(p t) o -> p (t o)", t=PACK))
             return tile
 
-        def load_plane(t):
-            tile = pool.tile([P, TABLE], F32, name="cq_plane%d" % t, tag="cq_plane%d" % t)
+        def load_cq_slice(t):
+            tile = pool.tile([P, TABLE], F32, name="cq_slice%d" % t, tag="cq_slice%d" % t)
             nc.sync.dma_start(tile[:], cq.rearrange("(p t) c -> p t c", t=PACK)[:, t, :])
             return tile
 
-        def flat(words):
+        def as_rows(words):
             return words[0].rearrange("p n t -> p (n t)")
 
+        def staged(stage, place):
+            return stage[STAGE + PACK * place : STAGE + PACK * (place + 1)]
+
         up_stage = pool.tile([P, PACK, HIDDEN // 4], I32, name="up_stage")
-        nc.vector.memset(up_stage[64:96], 0)
+        nc.vector.memset(up_stage[STAGE : STAGE + QUAD], 0)
         xo_plane = pool.tile([P, TABLE], U8, name="xo_plane")
         nc.vector.memset(xo_plane[:].bitcast(I32), 0)
         down_stage = pool.tile([P, PACK, OUT_ROWS // 4], I32, name="down_stage")
-        nc.vector.memset(down_stage[64:96], 0)
+        nc.vector.memset(down_stage[STAGE : STAGE + QUAD], 0)
 
         warm_in = pool.tile([P, 1], F32, name="warm_in")
         nc.vector.memset(warm_in[:], 0.0)
         warm_out = pool.tile([P, 1], F32, name="warm_out")
         nc.scalar.activation(warm_out[:], warm_in[:], SIGMOID)
-        planes = [load_plane(0)]
-        load_scale_rows(up_stage[64:68], w2_scales)
-        load_scale_rows(up_stage[68:72], w_scales)
+
+        cq_slices = [load_cq_slice(0)]
+        load_scale_rows(staged(up_stage, 0), w2_scales)
+        load_scale_rows(staged(up_stage, 1), w_scales)
         list1 = load_list(offs, "list1")
         xo_stage = pool.tile([PACK, PACK, TABLE // 4], I32, name="xo_stage")
         load_scale_rows(xo_stage[:], xo_scales)
         list2 = load_list(offs2, "list2")
-        xo_table = load_words(flat(xo_words), U32, TABLE, "xo_table")
-        planes.append(load_plane(1))
+        xo_table = load_words(as_rows(xo_words), U32, TABLE, "xo_table")
+        cq_slices.append(load_cq_slice(1))
         w2_raw = load_words(w2_words[0], U16, HIDDEN, "w2_raw")
-        planes.extend([load_plane(2), load_plane(3)])
+        cq_slices.extend([load_cq_slice(2), load_cq_slice(3)])
         list6 = load_list(offs6, "list6")
         list5 = load_list(offs5, "list5")
-        w_raw = load_words(flat(w_words), U32, HIDDEN, "w_raw")
-        load_scale_rows(down_stage[64:68], wb_scales)
-        load_scale_rows(down_stage[68:72], sx_scales)
-        load_scale_rows(down_stage[72:76], ws_scales)
+        w_raw = load_words(as_rows(w_words), U32, HIDDEN, "w_raw")
+        load_scale_rows(staged(down_stage, 0), wb_scales)
+        load_scale_rows(staged(down_stage, 1), sx_scales)
+        load_scale_rows(staged(down_stage, 2), ws_scales)
         list4 = load_list(offs4, "list4")
         list3 = load_list(offs3, "list3")
+        sa_cols = load_per_row(sa, "sa_cols", nc.sync)
         wb_codes = load_words(wb_words[0], U16, OUT_ROWS, "wb_codes")
-        ws_codes = load_words(flat(ws_words), U32, OUT_ROWS, "ws_codes")
-        sx_codes = load_words(flat(sx_words), U32, 2 * PLACES, "sx_codes")
+        ws_codes = load_words(as_rows(ws_words), U32, OUT_ROWS, "ws_codes")
+        sx_codes = load_words(as_rows(sx_words), U32, 2 * PLACES, "sx_codes")
         list7 = load_list(offs7, "list7")
-        gs_t = load_rows(gs, "gs_t")
-        sh_t = load_rows(sh, "sh_t")
-        bh_t = load_rows(bh, "bh_t")
-        sb_t = load_rows(sb, "sb_t")
-        sg_t = load_rows(sg, "sg_t")
-        bg_t = load_rows(bg, "bg_t")
-        sa_t = load_rows(sa, "sa_t")
+        gs_cols = load_per_row(gs, "gs_cols", nc.gpsimd)
+        sh_cols = load_per_row(sh, "sh_cols", nc.gpsimd)
+        bh_cols = load_per_row(bh, "bh_cols", nc.gpsimd)
+        sb_cols = load_per_row(sb, "sb_cols", nc.gpsimd)
+        sg_cols = load_per_row(sg, "sg_cols", nc.gpsimd)
+        bg_cols = load_per_row(bg, "bg_cols", nc.gpsimd)
 
         def spread(plane, stage, first, rows):
             for q in range(PACK):
@@ -112,29 +120,30 @@ def tile_list_gatedsides_codednote_further_scattered_kernel(
                     plane[QUAD * q : QUAD * q + rows, :].bitcast(I32), stage[first : first + rows, q, :]
                 )
 
+        def dealt(tile):
+            return tile[:].rearrange("p (m t) -> p t m", t=PACK)
+
+        def by_slice(tile):
+            return tile[:].rearrange("p (t m) -> p t m", t=PACK)
+
         spread(xo_plane, xo_stage, 0, PACK)
         up_raw = pool.tile([P, HIDDEN], U8, name="up_raw")
-        spread(up_raw, up_stage, 64, QUAD)
+        spread(up_raw, up_stage, STAGE, QUAD)
         xo_codes = pool.tile([P, SLOTS], U32, name="xo_codes", align_bytes=64)
         nc.vector.tensor_copy(xo_codes[:], xo_table[:].indirect(list2[:]))
         xo_picked = pool.tile([P, SLOTS], U8, name="xo_picked", align_bytes=64)
         nc.vector.tensor_copy(xo_picked[:], xo_plane[:].indirect(list2[:]))
         up_plane = pool.tile([P, HIDDEN], U8, name="up_plane", align_bytes=64)
-        nc.vector.tensor_copy(
-            up_plane[:].rearrange("p (t m) -> p t m", t=PACK), up_raw[:].rearrange("p (m t) -> p t m", t=PACK)
-        )
+        nc.vector.tensor_copy(by_slice(up_plane), dealt(up_raw))
         w2_codes = pool.tile([P, HIDDEN], U16, name="w2_codes", align_bytes=64)
-        nc.scalar.copy(
-            w2_codes[:].rearrange("p (t m) -> p t m", t=PACK), w2_raw[:].rearrange("p (m t) -> p t m", t=PACK)
-        )
+        nc.scalar.copy(by_slice(w2_codes), dealt(w2_raw))
 
         def first_stage(name, lhs_codes, lhs_dtype, lhs_plane, rhs_codes, rhs_plane):
             rows = []
             for t in range(PACK):
-                cols = slice(t * P, (t + 1) * P)
                 bank = psum.tile([P, SLOTS], F32, name="%s_bank%d" % (name, t), tag="bank%d" % t)
                 nc.tensor.matmul_mx(
-                    bank[:], lhsT=lhs_codes[:, cols].bitcast(lhs_dtype), lhsT_scale=lhs_plane[:, cols],
+                    bank[:], lhsT=lhs_codes[t].bitcast(lhs_dtype), lhsT_scale=lhs_plane[:, t * P : (t + 1) * P],
                     rhs=rhs_codes[:].bitcast(E4M3), rhs_scale=rhs_plane[:], start=True, stop=True,
                 )
                 tile = pool.tile([P, SLOTS], F32, name="%s%d" % (name, t), tag="%s%d" % (name, t), align_bytes=64)
@@ -164,31 +173,39 @@ def tile_list_gatedsides_codednote_further_scattered_kernel(
             nc.vector.quantize_mx(codes[:].bitcast(E5M2), plane[:], woven[:].rearrange("p o t -> p (o t)"))
             return codes, plane
 
-        b_rows = first_stage("b_rows", w2_codes, E2M1, up_plane, xo_codes, xo_picked)
+        w2_slices = [w2_codes[:, t * P : (t + 1) * P] for t in range(PACK)]
+        b_rows = first_stage("b_rows", w2_slices, E2M1, up_plane, xo_codes, xo_picked)
 
         x1_woven = pool.tile([P, SLOTS, PACK], BF16, name="x1_woven", tag="x1_woven", align_bytes=64)
         for pair in range(2):
-            picked = pool.tile([P, 2, SLOTS], BF16, name="x1_pair%d" % pair)
+            picked = pool.tile([P, 2, SLOTS], BF16, name="x1_pair%d" % pair, tag="x1_pair%d" % pair, align_bytes=64)
             for e in range(2):
                 t = 2 * pair + e
-                nc.scalar.activation(picked[:, e, :], planes[t][:].indirect(list1[:]), COPY, scale=gs_t[:, t : t + 1])
+                nc.scalar.activation(
+                    picked[:, e, :], cq_slices[t][:].indirect(list1[:]), COPY, scale=gs_cols[:, t : t + 1]
+                )
             nc.vector.tensor_copy(x1_woven[:, :, 2 * pair : 2 * pair + 2], picked[:].rearrange("p e j -> p j e"))
+
+        w_first = pool.tile([P, P], U32, name="w_first", align_bytes=64)
+        nc.vector.tensor_copy(w_first[:], dealt(w_raw)[:, 0, :])
         x1_codes = pool.tile([P, SLOTS], U32, name="x1_codes", tag="x1_codes", align_bytes=64)
         x1_plane = pool.tile([P, SLOTS], U8, name="x1_plane", align_bytes=64)
         nc.vector.quantize_mx(x1_codes[:].bitcast(E4M3), x1_plane[:], x1_woven[:].rearrange("p j t -> p (j t)"))
-        w_codes = pool.tile([P, HIDDEN], U32, name="w_codes", align_bytes=64)
-        nc.vector.tensor_copy(
-            w_codes[:].rearrange("p (t m) -> p t m", t=PACK), w_raw[:].rearrange("p (m t) -> p t m", t=PACK)
+        w_rest = pool.tile([P, PACK - 1, P], U32, name="w_rest", tag="x1_woven", align_bytes=64)
+        nc.vector.tensor_copy(w_rest[:], dealt(w_raw)[:, 1:, :])
+        w_slices = [w_first[:]] + [w_rest[:, t, :] for t in range(PACK - 1)]
+        a_rows = first_stage("a_rows", w_slices, E4M3, up_plane[PACK:], x1_codes, x1_plane)
+
+        h2_picks = pool.tile([P, 2, 2, 2, PLACES], F32, name="h2_picks", tag="cq_slice%d" % (PACK - 1))
+        h2_codes, h2_plane = gated(
+            "h2", b_rows, list5, sb_cols, list6, sh_cols, bh_cols, "x1_codes", (h2_picks[:, 0], h2_picks[:, 1])
         )
-        a_rows = first_stage("a_rows", w_codes, E4M3, up_plane[4:], x1_codes, x1_plane)
 
-        h2_picks = pool.tile([P, 2, 2, 2, PLACES], F32, name="h2_picks", tag="cq_plane3")
-        h2_codes, h2_plane = gated("h2", b_rows, list5, sb_t, list6, sh_t, bh_t, "x1_codes", (h2_picks[:, 0], h2_picks[:, 1]))
+        down_plane = pool.tile([P, OUT_ROWS], U8, name="down_plane", tag="x1_pair1", align_bytes=64)
+        spread(down_plane, down_stage, STAGE, QUAD)
 
-        down_plane = pool.tile([P, OUT_ROWS], U8, name="down_plane", tag="x1_woven", align_bytes=64)
-        spread(down_plane, down_stage, 64, QUAD)
         pages = []
-        for nt in range(2):
+        for nt in range(OUT_ROWS // P):
             page = pool.tile([P, PAGE], F32, name="page%d" % nt)
             nc.vector.memset(page[:], 0.0)
             pages.append(page)
@@ -197,34 +214,41 @@ def tile_list_gatedsides_codednote_further_scattered_kernel(
             d_cols = slice(half * PLACES, (half + 1) * PLACES)
             n_cols = slice(nt * P, (nt + 1) * P)
             nc.tensor.matmul_mx(
-                sums, lhsT=ws_codes[:, n_cols].bitcast(E4M3), lhsT_scale=down_plane[8:, n_cols],
-                rhs=sx_codes[:, d_cols].bitcast(E4M3), rhs_scale=down_plane[4:, d_cols], start=True, stop=False,
+                sums, lhsT=ws_codes[:, n_cols].bitcast(E4M3), lhsT_scale=down_plane[2 * PACK :, n_cols],
+                rhs=sx_codes[:, d_cols].bitcast(E4M3), rhs_scale=down_plane[PACK:, d_cols], start=True, stop=False,
             )
             nc.tensor.matmul_mx(
                 sums, lhsT=wb_codes[:, n_cols].bitcast(E2M1), lhsT_scale=down_plane[:, n_cols],
                 rhs=codes[:].bitcast(E5M2), rhs_scale=plane[:], start=False, stop=True,
             )
 
-        def places(half):
-            return list7[:, half * (PLACES // 16) : (half + 1) * (PLACES // 16)]
+        def columns_of(half):
+            return list7[:, half * (PLACES // PER_COLUMN) : (half + 1) * (PLACES // PER_COLUMN)]
 
         late_bank = psum.tile([P, 2, PLACES], F32, name="late_bank", tag="bank3")
         for nt in range(2):
-            second_stage(1, nt, h2_codes, h2_plane, late_bank[:, nt, :])
+            second_stage(LATE, nt, h2_codes, h2_plane, late_bank[:, nt, :])
         h1_picks = [pool.tile([P, 2, 2, PLACES], F32, name="h1_picks%d" % pair) for pair in range(2)]
-        h1_codes, h1_plane = gated("h1", a_rows, list3, sa_t, list4, sg_t, bg_t, "h1_woven", h1_picks)
+        h1_codes, h1_plane = gated("h1", a_rows, list3, sa_cols, list4, sg_cols, bg_cols, "h1_woven", h1_picks)
+
         late_result = pool.tile([P, 2, PLACES], F32, name="late_result", tag="a_rows3", align_bytes=64)
         nc.scalar.copy(late_result[:], late_bank[:])
         for nt in range(2):
-            nc.scalar.activation(pages[nt][:].indirect(places(1)), late_result[:, nt, :], COPY)
-        for nt in range(2):
+            nc.scalar.activation(pages[nt][:].indirect(columns_of(LATE)), late_result[:, nt, :], COPY)
+
+        def early_sums(nt):
             bank = psum.tile([P, PLACES], F32, name="early_bank%d" % nt, tag="bank%d" % (1 + nt))
-            second_stage(0, nt, h1_codes, h1_plane, bank[:])
-            result = pool.tile([P, PLACES], F32, name="early_result%d" % nt)
-            if nt == 0:
-                nc.vector.tensor_copy(result[:], bank[:])
-                nc.vector.tensor_copy(pages[nt][:].indirect(places(0)), result[:])
-            else:
-                nc.scalar.copy(result[:], bank[:])
-                nc.scalar.activation(pages[nt][:].indirect(places(0)), result[:], COPY)
-            nc.sync.dma_start(out[nt * P : (nt + 1) * P, :], pages[nt][:])
+            second_stage(EARLY, nt, h1_codes, h1_plane, bank[:])
+            return bank
+
+        bank0 = early_sums(0)
+        result0 = pool.tile([P, PLACES], F32, name="early_result0", tag="a_rows2", align_bytes=64)
+        nc.vector.tensor_copy(result0[:], bank0[:])
+        nc.vector.tensor_copy(pages[0][:].indirect(columns_of(EARLY)), result0[:])
+        nc.sync.dma_start(out[0:P, :], pages[0][:])
+
+        bank1 = early_sums(1)
+        result1 = pool.tile([P, PLACES], F32, name="early_result1", tag="a_rows3", align_bytes=64)
+        nc.scalar.copy(result1[:], bank1[:])
+        nc.scalar.activation(pages[1][:].indirect(columns_of(EARLY)), result1[:], COPY)
+        nc.sync.dma_start(out[P : 2 * P, :], pages[1][:])

@@ -78,11 +78,6 @@ def tile_list_gatedsides_codednote_further_scattered_kernel(
         down_stage = pool.tile([P, PACK, OUT_ROWS // 4], I32, name="down_stage")
         nc.vector.memset(down_stage[STAGE : STAGE + QUAD], 0)
 
-        warm_in = pool.tile([P, 1], F32, name="warm_in")
-        nc.vector.memset(warm_in[:], 0.0)
-        warm_out = pool.tile([P, 1], F32, name="warm_out")
-        nc.scalar.activation(warm_out[:], warm_in[:], SIGMOID)
-
         cq_slices = [load_cq_slice(0)]
         load_scale_rows(staged(up_stage, 0), w2_scales)
         load_scale_rows(staged(up_stage, 1), w_scales)

from contextlib import ExitStack

import concourse.mybir as mybir

F32 = mybir.dt.float32
BF16 = mybir.dt.bfloat16
I32 = mybir.dt.int32
U32 = mybir.dt.uint32
U16 = mybir.dt.uint16
U8 = mybir.dt.uint8
E4M3 = mybir.dt.float8_e4m3fn_x4
E5M2 = mybir.dt.float8_e5m2_x4
E2M1 = mybir.dt.float4_e2m1fn_x4
COPY = mybir.ActivationFunctionType.Copy
SIGMOID = mybir.ActivationFunctionType.Sigmoid
MULT = mybir.AluOpType.mult

P = 128
PACK = 4
QUAD = 32
CONTRACTION = P * PACK
TABLE = 1024
SLOTS = 256
HIDDEN = 512
PLACES = 128
OUT_ROWS = 256
PAGE = 1024
PER_COLUMN = 16
STAGE = 2 * QUAD
EARLY, LATE = 0, 1

FLOPS = 2 * CONTRACTION * (2 * HIDDEN * SLOTS + 2 * OUT_ROWS * 2 * PLACES)


def tile_list_gatedsides_codednote_further_scattered_kernel(
    tc, xo_words, xo_scales, cq, gs, w_words, w_scales, w2_words, w2_scales, sa, sb, sg, bg, sh, bh,
    wb_words, wb_scales, sx_words, sx_scales, ws_words, ws_scales,
    offs, offs2, offs3, offs4, offs5, offs6, offs7, out,
):
    nc = tc.nc
    with ExitStack() as ctx:
        pool = ctx.enter_context(tc.tile_pool(name="keep", bufs=1))
        psum = ctx.enter_context(tc.psum_pool(name="psum", bufs=1))

        def load_list(src, name):
            tile = pool.tile(list(src.shape), U16, name=name)
            nc.sync.dma_start(tile[:], src)
            return tile

        def load_words(src, dtype, columns, name):
            tile = pool.tile([P, columns], dtype, name=name, align_bytes=64)
            nc.sync.dma_start(tile[:].bitcast(I32), src.bitcast(I32))
            return tile

        def load_scale_rows(dst, src):
            nc.sync.dma_start(dst, src[0].bitcast(I32).rearrange("(q r) w -> r q w", r=PACK))

        def load_per_row(src, name, queue):
            tile = pool.tile([P, PACK], F32, name=name)
            queue.dma_start(tile[:], src.rearrange("(p t) o -> p (t o)", t=PACK))
            return tile

        def load_cq_slice(t):
            tile = pool.tile([P, TABLE], F32, name="cq_slice%d" % t, tag="cq_slice%d" % t)
            nc.sync.dma_start(tile[:], cq.rearrange("(p t) c -> p t c", t=PACK)[:, t, :])
            return tile

        def as_rows(words):
            return words[0].rearrange("p n t -> p (n t)")

        def staged(stage, place):
            return stage[STAGE + PACK * place : STAGE + PACK * (place + 1)]

        up_stage = pool.tile([P, PACK, HIDDEN // 4], I32, name="up_stage")
        nc.vector.memset(up_stage[STAGE : STAGE + QUAD], 0)
        xo_plane = pool.tile([P, TABLE], U8, name="xo_plane")
        nc.vector.memset(xo_plane[:].bitcast(I32), 0)
        down_stage = pool.tile([P, PACK, OUT_ROWS // 4], I32, name="down_stage")
        nc.vector.memset(down_stage[STAGE : STAGE + QUAD], 0)

        cq_slices = [load_cq_slice(0)]
        load_scale_rows(staged(up_stage, 0), w2_scales)
        load_scale_rows(staged(up_stage, 1), w_scales)
        list1 = load_list(offs, "list1")
        xo_stage = pool.tile([PACK, PACK, TABLE // 4], I32, name="xo_stage")
        load_scale_rows(xo_stage[:], xo_scales)
        list2 = load_list(offs2, "list2")
        xo_table = load_words(as_rows(xo_words), U32, TABLE, "xo_table")
        cq_slices.append(load_cq_slice(1))
        w2_raw = load_words(w2_words[0], U16, HIDDEN, "w2_raw")
        cq_slices.extend([load_cq_slice(2), load_cq_slice(3)])
        list6 = load_list(offs6, "list6")
        list5 = load_list(offs5, "list5")
        w_raw = load_words(as_rows(w_words), U32, HIDDEN, "w_raw")
        load_scale_rows(staged(down_stage, 0), wb_scales)
        load_scale_rows(staged(down_stage, 1), sx_scales)
        load_scale_rows(staged(down_stage, 2), ws_scales)
        list4 = load_list(offs4, "list4")
        list3 = load_list(offs3, "list3")
        sa_cols = load_per_row(sa, "sa_cols", nc.sync)
        wb_codes = load_words(wb_words[0], U16, OUT_ROWS, "wb_codes")
        ws_codes = load_words(as_rows(ws_words), U32, OUT_ROWS, "ws_codes")
        sx_codes = load_words(as_rows(sx_words), U32, 2 * PLACES, "sx_codes")
        list7 = load_list(offs7, "list7")
        gs_cols = load_per_row(gs, "gs_cols", nc.gpsimd)
        sh_cols = load_per_row(sh, "sh_cols", nc.gpsimd)
        bh_cols = load_per_row(bh, "bh_cols", nc.gpsimd)
        sb_cols = load_per_row(sb, "sb_cols", nc.gpsimd)
        sg_cols = load_per_row(sg, "sg_cols", nc.gpsimd)
        bg_cols = load_per_row(bg, "bg_cols", nc.gpsimd)

        def spread(plane, stage, first, rows):
            for q in range(PACK):
                nc.vector.tensor_copy(
                    plane[QUAD * q : QUAD * q + rows, :].bitcast(I32), stage[first : first + rows, q, :]
                )

        def dealt(tile):
            return tile[:].rearrange("p (m t) -> p t m", t=PACK)

        def by_slice(tile):
            return tile[:].rearrange("p (t m) -> p t m", t=PACK)

        spread(xo_plane, xo_stage, 0, PACK)
        up_raw = pool.tile([P, HIDDEN], U8, name="up_raw")
        spread(up_raw, up_stage, STAGE, QUAD)
        xo_codes = pool.tile([P, SLOTS], U32, name="xo_codes", align_bytes=64)
        nc.vector.tensor_copy(xo_codes[:], xo_table[:].indirect(list2[:]))
        xo_picked = pool.tile([P, SLOTS], U8, name="xo_picked", align_bytes=64)
        nc.vector.tensor_copy(xo_picked[:], xo_plane[:].indirect(list2[:]))
        up_plane = pool.tile([P, HIDDEN], U8, name="up_plane", align_bytes=64)
        nc.vector.tensor_copy(by_slice(up_plane), dealt(up_raw))
        w2_codes = pool.tile([P, HIDDEN], U16, name="w2_codes", align_bytes=64)
        nc.scalar.copy(by_slice(w2_codes), dealt(w2_raw))

        def first_stage(name, lhs_codes, lhs_dtype, lhs_plane, rhs_codes, rhs_plane):
            rows = []
            for t in range(PACK):
                bank = psum.tile([P, SLOTS], F32, name="%s_bank%d" % (name, t), tag="bank%d" % t)
                nc.tensor.matmul_mx(
                    bank[:], lhsT=lhs_codes[t].bitcast(lhs_dtype), lhsT_scale=lhs_plane[:, t * P : (t + 1) * P],
                    rhs=rhs_codes[:].bitcast(E4M3), rhs_scale=rhs_plane[:], start=True, stop=True,
                )
                tile = pool.tile([P, SLOTS], F32, name="%s%d" % (name, t), tag="%s%d" % (name, t), align_bytes=64)
                nc.vector.tensor_copy(tile[:], bank[:])
                rows.append(tile)
            return rows

        def gated(name, rows, value_list, weight, gate_list, slope, offset, woven_tag, picks):
            woven = pool.tile([P, PLACES, PACK], BF16, name=name + "_woven", tag=woven_tag, align_bytes=64)
            for pair in range(2):
                value, gate = picks[pair][:, 0], picks[pair][:, 1]
                for e in range(2):
                    t = 2 * pair + e
                    nc.scalar.activation(
                        gate[:, e, :], rows[t][:].indirect(gate_list[:]), SIGMOID,
                        bias=offset[:, t : t + 1], scale=slope[:, t : t + 1],
                    )
                    nc.scalar.activation(
                        value[:, e, :], rows[t][:].indirect(value_list[:]), COPY, scale=weight[:, t : t + 1]
                    )
                nc.vector.tensor_tensor(
                    woven[:, :, 2 * pair : 2 * pair + 2],
                    value.rearrange("p e o -> p o e"), gate.rearrange("p e o -> p o e"), MULT,
                )
            codes = pool.tile([P, PLACES], U32, name=name + "_codes", align_bytes=64)
            plane = pool.tile([P, PLACES], U8, name=name + "_plane", align_bytes=64)
            nc.vector.quantize_mx(codes[:].bitcast(E5M2), plane[:], woven[:].rearrange("p o t -> p (o t)"))
            return codes, plane

        w2_slices = [w2_codes[:, t * P : (t + 1) * P] for t in range(PACK)]
        b_rows = first_stage("b_rows", w2_slices, E2M1, up_plane, xo_codes, xo_picked)

        x1_woven = pool.tile([P, SLOTS, PACK], BF16, name="x1_woven", tag="x1_woven", align_bytes=64)
        for pair in range(2):
            picked = pool.tile([P, 2, SLOTS], BF16, name="x1_pair%d" % pair, tag="x1_pair%d" % pair, align_bytes=64)
            for e in range(2):
                t = 2 * pair + e
                nc.scalar.activation(
                    picked[:, e, :], cq_slices[t][:].indirect(list1[:]), COPY, scale=gs_cols[:, t : t + 1]
                )
            nc.vector.tensor_copy(x1_woven[:, :, 2 * pair : 2 * pair + 2], picked[:].rearrange("p e j -> p j e"))

        w_first = pool.tile([P, P], U32, name="w_first", align_bytes=64)
        nc.vector.tensor_copy(w_first[:], dealt(w_raw)[:, 0, :])
        x1_codes = pool.tile([P, SLOTS], U32, name="x1_codes", tag="x1_codes", align_bytes=64)
        x1_plane = pool.tile([P, SLOTS], U8, name="x1_plane", align_bytes=64)
        nc.vector.quantize_mx(x1_codes[:].bitcast(E4M3), x1_plane[:], x1_woven[:].rearrange("p j t -> p (j t)"))
        w_rest = pool.tile([P, PACK - 1, P], U32, name="w_rest", tag="x1_woven", align_bytes=64)
        nc.vector.tensor_copy(w_rest[:], dealt(w_raw)[:, 1:, :])
        w_slices = [w_first[:]] + [w_rest[:, t, :] for t in range(PACK - 1)]
        a_rows = first_stage("a_rows", w_slices, E4M3, up_plane[PACK:], x1_codes, x1_plane)

        h2_picks = pool.tile([P, 2, 2, 2, PLACES], F32, name="h2_picks", tag="cq_slice%d" % (PACK - 1))
        h2_codes, h2_plane = gated(
            "h2", b_rows, list5, sb_cols, list6, sh_cols, bh_cols, "x1_codes", (h2_picks[:, 0], h2_picks[:, 1])
        )

        down_plane = pool.tile([P, OUT_ROWS], U8, name="down_plane", tag="x1_pair1", align_bytes=64)
        spread(down_plane, down_stage, STAGE, QUAD)

        pages = []
        for nt in range(OUT_ROWS // P):
            page = pool.tile([P, PAGE], F32, name="page%d" % nt)
            nc.vector.memset(page[:], 0.0)
            pages.append(page)

        def second_stage(half, nt, codes, plane, sums):
            d_cols = slice(half * PLACES, (half + 1) * PLACES)
            n_cols = slice(nt * P, (nt + 1) * P)
            nc.tensor.matmul_mx(
                sums, lhsT=ws_codes[:, n_cols].bitcast(E4M3), lhsT_scale=down_plane[2 * PACK :, n_cols],
                rhs=sx_codes[:, d_cols].bitcast(E4M3), rhs_scale=down_plane[PACK:, d_cols], start=True, stop=False,
            )
            nc.tensor.matmul_mx(
                sums, lhsT=wb_codes[:, n_cols].bitcast(E2M1), lhsT_scale=down_plane[:, n_cols],
                rhs=codes[:].bitcast(E5M2), rhs_scale=plane[:], start=False, stop=True,
            )

        def columns_of(half):
            return list7[:, half * (PLACES // PER_COLUMN) : (half + 1) * (PLACES // PER_COLUMN)]

        late_bank = psum.tile([P, 2, PLACES], F32, name="late_bank", tag="bank3")
        for nt in range(2):
            second_stage(LATE, nt, h2_codes, h2_plane, late_bank[:, nt, :])
        h1_picks = [pool.tile([P, 2, 2, PLACES], F32, name="h1_picks%d" % pair) for pair in range(2)]
        h1_codes, h1_plane = gated("h1", a_rows, list3, sa_cols, list4, sg_cols, bg_cols, "h1_woven", h1_picks)

        late_result = pool.tile([P, 2, PLACES], F32, name="late_result", tag="a_rows3", align_bytes=64)
        nc.scalar.copy(late_result[:], late_bank[:])
        for nt in range(2):
            nc.scalar.activation(pages[nt][:].indirect(columns_of(LATE)), late_result[:, nt, :], COPY)

        def early_sums(nt):
            bank = psum.tile([P, PLACES], F32, name="early_bank%d" % nt, tag="bank%d" % (1 + nt))
            second_stage(EARLY, nt, h1_codes, h1_plane, bank[:])
            return bank

        bank0 = early_sums(0)
        result0 = pool.tile([P, PLACES], F32, name="early_result0", tag="a_rows2", align_bytes=64)
        nc.vector.tensor_copy(result0[:], bank0[:])
        nc.vector.tensor_copy(pages[0][:].indirect(columns_of(EARLY)), result0[:])
        nc.sync.dma_start(out[0:P, :], pages[0][:])

        bank1 = early_sums(1)
        result1 = pool.tile([P, PLACES], F32, name="early_result1", tag="a_rows3", align_bytes=64)
        nc.scalar.copy(result1[:], bank1[:])
        nc.scalar.activation(pages[1][:].indirect(columns_of(EARLY)), result1[:], COPY)
        nc.sync.dma_start(out[P : 2 * P, :], pages[1][:])
